import numpy as np
import ml_dtypes


def mxq(x, axis, fmt="e4m3"):
    dtype, down = {"e4m3": (ml_dtypes.float8_e4m3fn, 7), "e5m2": (ml_dtypes.float8_e5m2, 14)}[fmt]
    v = np.moveaxis(np.asarray(x, np.float32).astype(ml_dtypes.bfloat16).astype(np.float64), axis, -1)
    blocks = v.reshape(v.shape[:-1] + (-1, 32))
    amax = np.abs(blocks).max(-1, keepdims=True)
    byte = np.maximum(np.where(amax > 0, np.frexp(amax)[1] - 1 + 127, 0) - down, 1)
    scale = np.exp2(byte - 127.0)
    codes = (blocks / scale).astype(np.float32).astype(dtype).astype(np.float64)
    return np.moveaxis((codes * scale).reshape(v.shape), -1, axis)


WIDE = False


def mx_kscale(k):
    if not WIDE:
        return np.ones(k)
    levels = np.array([10, -10, 5, -5, 0])
    if k % 512:
        return np.exp2(np.random.permutation(np.resize(levels, k // 32))).repeat(32)
    a = np.empty((k // 512, 16))
    for p in range(k // 512):
        a[p, :8] = np.random.permutation(np.resize(levels, 8))
        for g in range(8):
            far = levels[np.abs(levels - a[p, g]) >= 10]
            a[p, g + 8] = far[np.random.randint(len(far))]
    return np.exp2(a.ravel()).repeat(32)


def f64(x):
    return np.asarray(x).astype(np.float64)


def striped(idx):
    return np.tile(idx.reshape(-1, 16).T, (8, 1)).astype(np.uint16)


def unstriped(offs):
    return offs[:16].T.reshape(-1).astype(np.int64)


def pack_weight(w):
    k, n = w.shape
    w = f64(np.asarray(w, np.float32).astype(ml_dtypes.bfloat16)).reshape(k // 32, 32, n)
    amax = np.abs(w).max(1)
    byte = np.clip(np.where(amax > 0, np.frexp(amax)[1] - 1 + 127 - 7, 1), 1, 254)
    scaled = (w * np.exp2(127.0 - byte)[:, None, :]).reshape(k, n).astype(np.float32)
    words = np.ascontiguousarray(scaled.reshape(k // 512, 128, 4, n).transpose(0, 1, 3, 2)).astype(ml_dtypes.float8_e4m3fn).view(np.uint8)
    return words, np.ascontiguousarray(byte.astype(np.uint8).reshape(k // 512, 16, n))


def unpack_weight(words, scales):
    g, p, n, _ = words.shape
    vals = np.ascontiguousarray(words).view(ml_dtypes.float8_e4m3fn).astype(np.float64) * np.repeat(np.exp2(scales.astype(np.float64) - 127.0), 8, axis=1)[..., None]
    return vals.transpose(0, 1, 3, 2).reshape(g * 512, n)


K, T, D, N = 1024, 512, 3, 256
P = 2 ** 7


def setup_inputs():
    n = np.random.standard_normal
    s = mx_kscale(K)[:, None]
    packed_xT = pack_weight(n((K, T)) * s)
    return {
        "x_words": packed_xT[0],
        "x_scales": packed_xT[1],
        "w1": (n((K, N)) / np.sqrt(K) / s).astype(np.float32),
        "score": np.tile(np.random.standard_normal((D, 1, T)), (1, P, 1)).astype(np.float32),
        "pos1": striped(np.random.permutation(T)),
        "pos2": striped(np.random.permutation(T)),
        "pos3": striped(np.random.permutation(T)),
    }


def reference(x_words, x_scales, w1, score, pos1, pos2, pos3):
    xq = unpack_weight(x_words, x_scales)
    y = mxq(f64(w1), 0, "e4m3").T @ xq
    e0 = np.exp(f64(score)[0, :1])
    e1 = np.exp(f64(score)[1, :1])
    e2 = np.exp(f64(score)[2, :1])
    num = y[:, unstriped(pos1)] * e0 + y[:, unstriped(pos2)] * e1 + y[:, unstriped(pos3)] * e2
    den = e0 + e1 + e2
    return num / den

@@ -1,0 +1,211 @@
+from contextlib import ExitStack
+
+import concourse.mybir as mybir
+from concourse.masks import make_identity
+
+K, T, D, N = 1024, 512, 3, 256
+FLOPS = 2 * K * N * T
+BYTES = K * T + K * T // 32 + 4 * K * N + 4 * D * T + 2 * D * 128 * T // 16 + 4 * N * T
+
+F32 = mybir.dt.float32
+BF16 = mybir.dt.bfloat16
+I32 = mybir.dt.int32
+U32 = mybir.dt.uint32
+U16 = mybir.dt.uint16
+U8 = mybir.dt.uint8
+FP8X4 = mybir.dt.float8_e4m3fn_x4
+ALU = mybir.AluOpType
+ACT = mybir.ActivationFunctionType
+AXIS_X = mybir.AxisListType.X
+
+P = 128
+PACK = 4
+K_PASS = P * PACK
+PASSES = K // K_PASS
+HALF = T // 2
+SPARE = 16
+PER_PART = T // P
+
+
+def tile_picked_wgatv_none_l_kernel(
+    tc, x_words, x_scales, w1, score, pos1, pos2, pos3, out
+):
+    nc = tc.nc
+    with ExitStack() as ctx:
+        keep = ctx.enter_context(tc.tile_pool(name="keep", bufs=1))
+        psum = ctx.enter_context(tc.psum_pool(name="psum", bufs=1))
+
+        sc = keep.tile([P, D, PER_PART], F32, name="sc")
+        nc.sync.dma_start(out=sc[:], in_=score[:, 0, :].rearrange("d (p c) -> p d c", c=PER_PART))
+
+        x_plane = keep.tile([P, PASSES, T], U8, name="x_plane", align_bytes=64)
+        nc.gpsimd.memset(x_plane[:].bitcast(I32), 0)
+        plane_rows = x_scales.rearrange("g (q r) c -> r q g c", r=4)
+
+        w_raw = []
+        x_codes = []
+        for g in range(PASSES):
+            w_raw.append(keep.tile([P, PACK, N], F32, name="w_raw_%d" % g))
+            rows = w1[g * K_PASS : (g + 1) * K_PASS, :]
+            nc.sync.dma_start(out=w_raw[g][:], in_=rows.rearrange("(p j) n -> p j n", j=PACK))
+            if g == 0:
+                for r in range(4):
+                    nc.sync.dma_start(out=x_plane[r:P:32, :, :].bitcast(I32), in_=plane_rows[r].bitcast(I32))
+            x_codes.append(keep.tile([P, T], U32, name="x_codes_%d" % g, align_bytes=64))
+            nc.sync.dma_start(
+                out=x_codes[g][:].bitcast(I32), in_=x_words[g].rearrange("p n t -> p (n t)").bitcast(I32)
+            )
+        lists = [keep.tile([P, T // 16], U16, name="list_%d" % d) for d in range(D)]
+        nc.sync.dma_start(lists[0][:], pos1)
+        nc.sync.dma_start(lists[1][:], pos2)
+        nc.sync.dma_start(lists[2][:], pos3)
+
+        ident = keep.tile([P, P], F32, name="ident")
+        make_identity(nc, ident[:])
+        y = [keep.tile([P, T + SPARE], F32, name="y_%d" % m) for m in range(2)]
+        for m in range(2):
+            nc.gpsimd.memset(y[m][:, T:], 0.0)
+
+        warm = keep.tile([P, 2], F32, name="warm")
+        nc.vector.memset(warm[:, 0:1], 0.0)
+        nc.scalar.activation(out=warm[:, 1:2], in_=warm[:, 0:1], func=ACT.Exp)
+
+        mx = keep.tile([P, PER_PART], F32, name="mx")
+        nc.vector.tensor_reduce(out=mx[:], in_=sc[:].rearrange("p d c -> p c d"), axis=AXIS_X, op=ALU.max)
+        sh = keep.tile([P, D, PER_PART], F32, name="sh")
+        nc.vector.tensor_tensor(
+            out=sh[:], in0=sc[:], in1=mx[:].unsqueeze(1).to_broadcast([P, D, PER_PART]), op=ALU.subtract
+        )
+        ex = keep.tile([P, D, PER_PART], F32, name="ex")
+        nc.scalar.activation(out=ex[:], in_=sh[:], func=ACT.Exp)
+        den = keep.tile([P, PER_PART], F32, name="den")
+        nc.vector.tensor_reduce(out=den[:], in_=ex[:].rearrange("p d c -> p c d"), axis=AXIS_X, op=ALU.add)
+        rec = keep.tile([P, PER_PART], F32, name="rec", tag="w_codes_0_1", align_bytes=64)
+        nc.vector.reciprocal(out=rec[:], in_=den[:])
+        att = keep.tile([P, D, PER_PART], F32, name="att")
+        nc.vector.tensor_tensor(
+            out=att[:], in0=ex[:], in1=rec[:].unsqueeze(1).to_broadcast([P, D, PER_PART]), op=ALU.mult
+        )
+
+        a_rows = [keep.tile([P, T], F32, name="a_rows_%d" % d) for d in range(D)]
+
+        def spread(d, on_vector, tag):
+            bank = psum.tile([P, PER_PART, P], F32, name="a_bank_%d" % d, tag=tag)
+            for c in range(PER_PART):
+                nc.tensor.transpose(bank[:, c, :], att[:, d, c : c + 1].to_broadcast([P, P]), ident[:])
+            dst = a_rows[d][:].rearrange("i (p c) -> i p c", c=PER_PART)
+            src = bank[:].rearrange("i c p -> i p c")
+            if on_vector:
+                nc.vector.tensor_copy(out=dst, in_=src)
+            else:
+                nc.scalar.copy(out=dst, in_=src)
+
+        w_bf = {}
+        w_codes = {}
+        w_plane = {}
+
+        def cast_w(m, g, on_vector):
+            w_bf[m, g] = keep.tile([P, P, PACK], BF16, name="w_bf_%d_%d" % (m, g), tag="w_bf_%d" % m, align_bytes=64)
+            dst = w_bf[m, g][:].rearrange("p (c i) t -> p c t i", i=4)
+            src = w_raw[g][:, :, m * P : (m + 1) * P].rearrange("p t (c i) -> p c t i", i=4)
+            if on_vector:
+                nc.vector.tensor_copy(out=dst, in_=src)
+            else:
+                nc.scalar.copy(out=dst, in_=src)
+
+        def quantize_w(m, g):
+            w_codes[m, g] = keep.tile([P, P], U32, name="w_codes_%d_%d" % (m, g), tag="w_codes_%d_%d" % (m, g), align_bytes=64)
+            w_plane[m, g] = keep.tile([P, P], U8, name="w_plane_%d_%d" % (m, g), align_bytes=64)
+            nc.vector.quantize_mx(
+                out=w_codes[m, g][:].bitcast(FP8X4),
+                scales=w_plane[m, g][:],
+                in_=w_bf[m, g][:].rearrange("p w j -> p (w j)"),
+            )
+
+        def project(m, halves):
+            banks = {h: psum.tile([P, HALF], F32, name="y_bank_%d_%d" % (m, h), tag=tag) for h, tag in halves}
+            for g in range(PASSES):
+                for h in banks:
+                    cols = slice(h * HALF, (h + 1) * HALF)
+                    nc.tensor.matmul_mx(
+                        out=banks[h][:],
+                        lhsT=w_codes[m, g][:].bitcast(FP8X4),
+                        lhsT_scale=w_plane[m, g][:],
+                        rhs=x_codes[g][:, cols].bitcast(FP8X4),
+                        rhs_scale=x_plane[:, g, cols],
+                        start=(g == 0),
+                        stop=(g == PASSES - 1),
+                    )
+            for h in banks:
+                cols = slice(h * HALF, (h + 1) * HALF)
+                if (m, h) == (0, 1):
+                    nc.vector.tensor_copy(out=y[m][:, cols], in_=banks[h][:])
+                else:
+                    nc.scalar.copy(out=y[m][:, cols], in_=banks[h][:])
+
+        def gather(m, d, lo, hi):
+            term = keep.tile([P, hi - lo], F32, name="term_%d_%d_%d" % (m, d, lo))
+            nc.vector.tensor_tensor(
+                out=term[:],
+                in0=y[m][:].indirect(lists[d][:, lo // 16 : hi // 16]),
+                in1=a_rows[d][:, lo:hi],
+                op=ALU.mult,
+            )
+            return term
+
+        def add_turned(bank, term, first, last):
+            chunks = term.shape[1] // P
+            for c in range(chunks):
+                nc.tensor.matmul(
+                    out=bank[:, c * P : (c + 1) * P],
+                    lhsT=term[:, c * P : (c + 1) * P],
+                    rhs=ident[:],
+                    is_transpose=True,
+                    start=(first and c == 0),
+                    stop=(last and c == chunks - 1),
+                )
+
+        def turn_back(bank, width, name, tag):
+            turned = keep.tile([P, width], F32, name="turned_" + name)
+            nc.scalar.copy(out=turned[:], in_=bank[:])
+            back = psum.tile([P, width], F32, name="back_" + name, tag=tag)
+            for c in range(width // P):
+                nc.tensor.transpose(back[:, c * P : (c + 1) * P], turned[:, c * P : (c + 1) * P], ident[:])
+            return back
+
+        for g in range(PASSES):
+            for m in range(2):
+                cast_w(m, g, g == 1)
+                quantize_w(m, g)
+        spread(0, False, "bank_a")
+        project(0, [(0, "bank_b"), (1, "bank_c")])
+        spread(1, False, "bank_b")
+        spread(2, False, "bank_c")
+        project(1, [(0, "bank_a")])
+        project(1, [(1, "bank_b")])
+
+        sum0 = psum.tile([P, T], F32, name="sum0", tag="sum0")
+        term = gather(0, 0, 0, T)
+        add_turned(sum0, term, True, False)
+        term = gather(0, 1, 0, T)
+        add_turned(sum0, term, False, False)
+        term = gather(0, 2, 0, T)
+        add_turned(sum0, term, False, True)
+        back0 = turn_back(sum0, T, "0", "bank_d")
+        res0 = keep.tile([P, T], F32, name="res0")
+        nc.scalar.copy(out=res0[:], in_=back0[:])
+        nc.sync.dma_start(out=out[0:P, :], in_=res0[:])
+
+        backs = []
+        for h in range(2):
+            lo, hi = h * HALF, (h + 1) * HALF
+            part = psum.tile([P, HALF], F32, name="sum1_%d" % h, tag=("bank_g", "sum0")[h])
+            for d in range(2):
+                term = gather(1, d, lo, hi)
+                add_turned(part, term, d == 0, d == 1)
+            backs.append(turn_back(part, HALF, "1_%d" % h, ("bank_e", "bank_f")[h]))
+        last = [gather(1, 2, h * HALF, (h + 1) * HALF) for h in range(2)]
+        for h in range(2):
+            res1 = keep.tile([P, HALF], F32, name="res1_%d" % h)
+            nc.vector.tensor_tensor(out=res1[:], in0=backs[h][:], in1=last[h][:], op=ALU.add)
+            nc.sync.dma_start(out=out[P : 2 * P, h * HALF : (h + 1) * HALF], in_=res1[:])

@@ -42,23 +42,26 @@ def tile_picked_wgatv_none_l_kernel(
         nc.gpsimd.memset(x_plane[:].bitcast(I32), 0)
         plane_rows = x_scales.rearrange("g (q r) c -> r q g c", r=4)
 
-        w_raw = []
-        x_codes = []
-        for g in range(PASSES):
-            w_raw.append(keep.tile([P, PACK, N], F32, name="w_raw_%d" % g))
-            rows = w1[g * K_PASS : (g + 1) * K_PASS, :]
-            nc.sync.dma_start(out=w_raw[g][:], in_=rows.rearrange("(p j) n -> p j n", j=PACK))
-            if g == 0:
-                for r in range(4):
-                    nc.sync.dma_start(out=x_plane[r:P:32, :, :].bitcast(I32), in_=plane_rows[r].bitcast(I32))
-            x_codes.append(keep.tile([P, T], U32, name="x_codes_%d" % g, align_bytes=64))
-            nc.sync.dma_start(
-                out=x_codes[g][:].bitcast(I32), in_=x_words[g].rearrange("p n t -> p (n t)").bitcast(I32)
-            )
+        w_raw = {}
         lists = [keep.tile([P, T // 16], U16, name="list_%d" % d) for d in range(D)]
-        nc.sync.dma_start(lists[0][:], pos1)
-        nc.sync.dma_start(lists[1][:], pos2)
-        nc.sync.dma_start(lists[2][:], pos3)
+
+        def load_w(m, g):
+            w_raw[m, g] = keep.tile([P, PACK, P], F32, name="w_raw_%d_%d" % (m, g))
+            rows = w1[g * K_PASS : (g + 1) * K_PASS, m * P : (m + 1) * P]
+            nc.sync.dma_start(out=w_raw[m, g][:], in_=rows.rearrange("(p j) n -> p j n", j=PACK))
+
+        load_w(0, 0)
+        for r in range(4):
+            nc.sync.dma_start(out=x_plane[r:P:32, :, :].bitcast(I32), in_=plane_rows[r].bitcast(I32))
+        load_w(0, 1)
+        x_codes = keep.tile([P, PASSES, T], U32, name="x_codes", align_bytes=64)
+        nc.sync.dma_start(
+            out=x_codes[:].bitcast(I32), in_=x_words.rearrange("g p n t -> p g (n t)").bitcast(I32)
+        )
+        load_w(1, 0)
+        load_w(1, 1)
+        for d, pos in enumerate((pos1, pos2, pos3)):
+            nc.sync.dma_start(lists[d][:], pos)
 
         ident = keep.tile([P, P], F32, name="ident")
         make_identity(nc, ident[:])
@@ -72,7 +75,7 @@ def tile_picked_wgatv_none_l_kernel(
 
         mx = keep.tile([P, PER_PART], F32, name="mx")
         nc.vector.tensor_reduce(out=mx[:], in_=sc[:].rearrange("p d c -> p c d"), axis=AXIS_X, op=ALU.max)
-        sh = keep.tile([P, D, PER_PART], F32, name="sh")
+        sh = keep.tile([P, D, PER_PART], F32, name="sh", tag="w_bf_0_0", align_bytes=64)
         nc.vector.tensor_tensor(
             out=sh[:], in0=sc[:], in1=mx[:].unsqueeze(1).to_broadcast([P, D, PER_PART]), op=ALU.subtract
         )
@@ -82,10 +85,6 @@ def tile_picked_wgatv_none_l_kernel(
         nc.vector.tensor_reduce(out=den[:], in_=ex[:].rearrange("p d c -> p c d"), axis=AXIS_X, op=ALU.add)
         rec = keep.tile([P, PER_PART], F32, name="rec", tag="w_codes_0_1", align_bytes=64)
         nc.vector.reciprocal(out=rec[:], in_=den[:])
-        att = keep.tile([P, D, PER_PART], F32, name="att")
-        nc.vector.tensor_tensor(
-            out=att[:], in0=ex[:], in1=rec[:].unsqueeze(1).to_broadcast([P, D, PER_PART]), op=ALU.mult
-        )
 
         a_rows = [keep.tile([P, T], F32, name="a_rows_%d" % d) for d in range(D)]
 
@@ -100,27 +99,25 @@ def tile_picked_wgatv_none_l_kernel(
             else:
                 nc.scalar.copy(out=dst, in_=src)
 
-        w_bf = {}
         w_codes = {}
         w_plane = {}
 
-        def cast_w(m, g, on_vector):
-            w_bf[m, g] = keep.tile([P, P, PACK], BF16, name="w_bf_%d_%d" % (m, g), tag="w_bf_%d" % m, align_bytes=64)
-            dst = w_bf[m, g][:].rearrange("p (c i) t -> p c t i", i=4)
-            src = w_raw[g][:, :, m * P : (m + 1) * P].rearrange("p t (c i) -> p c t i", i=4)
-            if on_vector:
+        def cast_w(m, g, dst):
+            dst = dst.rearrange("p (c i t) -> p c t i", i=4, t=PACK)
+            src = w_raw[m, g][:].rearrange("p t (c i) -> p c t i", i=4)
+            if m == 1:
                 nc.vector.tensor_copy(out=dst, in_=src)
             else:
                 nc.scalar.copy(out=dst, in_=src)
 
-        def quantize_w(m, g):
-            w_codes[m, g] = keep.tile([P, P], U32, name="w_codes_%d_%d" % (m, g), tag="w_codes_%d_%d" % (m, g), align_bytes=64)
-            w_plane[m, g] = keep.tile([P, P], U8, name="w_plane_%d_%d" % (m, g), align_bytes=64)
-            nc.vector.quantize_mx(
-                out=w_codes[m, g][:].bitcast(FP8X4),
-                scales=w_plane[m, g][:],
-                in_=w_bf[m, g][:].rearrange("p w j -> p (w j)"),
-            )
+        def quantize_w(m, passes, staged):
+            name = "%d_%d" % (m, passes[0])
+            codes = keep.tile([P, len(passes) * P], U32, name="w_codes_" + name, tag="w_codes_" + name, align_bytes=64)
+            plane = keep.tile([P, len(passes) * P], U8, name="w_plane_" + name, align_bytes=64)
+            nc.vector.quantize_mx(out=codes[:].bitcast(FP8X4), scales=plane[:], in_=staged[:])
+            for j, g in enumerate(passes):
+                w_codes[m, g] = codes[:, j * P : (j + 1) * P]
+                w_plane[m, g] = plane[:, j * P : (j + 1) * P]
 
         def project(m, halves):
             banks = {h: psum.tile([P, HALF], F32, name="y_bank_%d_%d" % (m, h), tag=tag) for h, tag in halves}
@@ -129,9 +126,9 @@ def tile_picked_wgatv_none_l_kernel(
                     cols = slice(h * HALF, (h + 1) * HALF)
                     nc.tensor.matmul_mx(
                         out=banks[h][:],
-                        lhsT=w_codes[m, g][:].bitcast(FP8X4),
-                        lhsT_scale=w_plane[m, g][:],
-                        rhs=x_codes[g][:, cols].bitcast(FP8X4),
+                        lhsT=w_codes[m, g].bitcast(FP8X4),
+                        lhsT_scale=w_plane[m, g],
+                        rhs=x_codes[:, g, cols].bitcast(FP8X4),
                         rhs_scale=x_plane[:, g, cols],
                         start=(g == 0),
                         stop=(g == PASSES - 1),
@@ -173,10 +170,22 @@ def tile_picked_wgatv_none_l_kernel(
                 nc.tensor.transpose(back[:, c * P : (c + 1) * P], turned[:, c * P : (c + 1) * P], ident[:])
             return back
 
+        staged = [
+            keep.tile([P, K_PASS], BF16, name="w_bf_0_%d" % g, tag="w_bf_0_%d" % g, align_bytes=64)
+            for g in range(PASSES)
+        ]
         for g in range(PASSES):
-            for m in range(2):
-                cast_w(m, g, g == 1)
-                quantize_w(m, g)
+            cast_w(0, g, staged[g][:])
+        att = keep.tile([P, D, PER_PART], F32, name="att")
+        nc.vector.tensor_tensor(
+            out=att[:], in0=ex[:], in1=rec[:].unsqueeze(1).to_broadcast([P, D, PER_PART]), op=ALU.mult
+        )
+        quantize_w(0, [0], staged[0])
+        quantize_w(0, [1], staged[1])
+        staged_1 = keep.tile([P, PASSES * K_PASS], BF16, name="w_bf_1", tag="w_bf_0_1", align_bytes=64)
+        for g in range(PASSES):
+            cast_w(1, g, staged_1[:, g * K_PASS : (g + 1) * K_PASS])
+        quantize_w(1, [0, 1], staged_1)
         spread(0, False, "bank_a")
         project(0, [(0, "bank_b"), (1, "bank_c")])
         spread(1, False, "bank_b")
@@ -194,18 +203,15 @@ def tile_picked_wgatv_none_l_kernel(
         back0 = turn_back(sum0, T, "0", "bank_d")
         res0 = keep.tile([P, T], F32, name="res0")
         nc.scalar.copy(out=res0[:], in_=back0[:])
-        nc.sync.dma_start(out=out[0:P, :], in_=res0[:])
+        nc.scalar.dma_start(out=out[0:P, :], in_=res0[:])
 
-        backs = []
+        terms = [gather(1, d, 0, T) for d in range(2)]
+        last = [gather(1, 2, 0, HALF)]
+        pair = keep.tile([P, T], F32, name="pair")
+        nc.vector.tensor_tensor(out=pair[:], in0=terms[0][:], in1=terms[1][:], op=ALU.add)
+        last.append(gather(1, 2, HALF, T))
         for h in range(2):
-            lo, hi = h * HALF, (h + 1) * HALF
-            part = psum.tile([P, HALF], F32, name="sum1_%d" % h, tag=("bank_g", "sum0")[h])
-            for d in range(2):
-                term = gather(1, d, lo, hi)
-                add_turned(part, term, d == 0, d == 1)
-            backs.append(turn_back(part, HALF, "1_%d" % h, ("bank_e", "bank_f")[h]))
-        last = [gather(1, 2, h * HALF, (h + 1) * HALF) for h in range(2)]
-        for h in range(2):
+            cols = slice(h * HALF, (h + 1) * HALF)
             res1 = keep.tile([P, HALF], F32, name="res1_%d" % h)
-            nc.vector.tensor_tensor(out=res1[:], in0=backs[h][:], in1=last[h][:], op=ALU.add)
-            nc.sync.dma_start(out=out[P : 2 * P, h * HALF : (h + 1) * HALF], in_=res1[:])
+            nc.vector.tensor_tensor(out=res1[:], in0=pair[:, cols], in1=last[h][:], op=ALU.add)
+            nc.sync.dma_start(out=out[P : 2 * P, cols], in_=res1[:])

@@ -64,10 +64,11 @@ def tile_picked_wgatv_none_l_kernel(
             nc.sync.dma_start(lists[d][:], pos)
 
         ident = keep.tile([P, P], F32, name="ident")
-        make_identity(nc, ident[:])
+        nc.vector.memset(ident[:], 0.0)
+        make_identity(nc, ident[:], nomemset=True)
         y = [keep.tile([P, T + SPARE], F32, name="y_%d" % m) for m in range(2)]
         for m in range(2):
-            nc.gpsimd.memset(y[m][:, T:], 0.0)
+            nc.vector.memset(y[m][:, T:], 0.0)
 
         warm = keep.tile([P, 2], F32, name="warm")
         nc.vector.memset(warm[:, 0:1], 0.0)
@@ -91,7 +92,7 @@ def tile_picked_wgatv_none_l_kernel(
         def spread(d, on_vector, tag):
             bank = psum.tile([P, PER_PART, P], F32, name="a_bank_%d" % d, tag=tag)
             for c in range(PER_PART):
-                nc.tensor.transpose(bank[:, c, :], att[:, d, c : c + 1].to_broadcast([P, P]), ident[:])
+                nc.tensor.transpose(bank[:, c, :], att[d][c].to_broadcast([P, P]), ident[:])
             dst = a_rows[d][:].rearrange("i (p c) -> i p c", c=PER_PART)
             src = bank[:].rearrange("i c p -> i p c")
             if on_vector:
@@ -114,7 +115,7 @@ def tile_picked_wgatv_none_l_kernel(
             name = "%d_%d" % (m, passes[0])
             codes = keep.tile([P, len(passes) * P], U32, name="w_codes_" + name, tag="w_codes_" + name, align_bytes=64)
             plane = keep.tile([P, len(passes) * P], U8, name="w_plane_" + name, align_bytes=64)
-            nc.vector.quantize_mx(out=codes[:].bitcast(FP8X4), scales=plane[:], in_=staged[:])
+            nc.vector.quantize_mx(out=codes[:].bitcast(FP8X4), scales=plane[:], in_=staged)
             for j, g in enumerate(passes):
                 w_codes[m, g] = codes[:, j * P : (j + 1) * P]
                 w_plane[m, g] = plane[:, j * P : (j + 1) * P]
@@ -176,25 +177,30 @@ def tile_picked_wgatv_none_l_kernel(
         ]
         for g in range(PASSES):
             cast_w(0, g, staged[g][:])
-        att = keep.tile([P, D, PER_PART], F32, name="att")
+        att_lead = keep.tile([P, 1], F32, name="att_lead", tag="w_codes_0_0", align_bytes=64)
+        nc.vector.tensor_tensor(out=att_lead[:], in0=ex[:, 0, 0:1], in1=rec[:, 0:1], op=ALU.mult)
+        att_first = keep.tile([P, PER_PART - 1], F32, name="att_first")
+        nc.vector.tensor_tensor(out=att_first[:], in0=ex[:, 0, 1:], in1=rec[:, 1:], op=ALU.mult)
+        att_rest = keep.tile([P, D - 1, PER_PART], F32, name="att_rest")
         nc.vector.tensor_tensor(
-            out=att[:], in0=ex[:], in1=rec[:].unsqueeze(1).to_broadcast([P, D, PER_PART]), op=ALU.mult
+            out=att_rest[:], in0=ex[:, 1:, :], in1=rec[:].unsqueeze(1).to_broadcast([P, D - 1, PER_PART]), op=ALU.mult
         )
-        quantize_w(0, [0], staged[0])
-        quantize_w(0, [1], staged[1])
+        att = [[att_lead[:]] + [att_first[:, c : c + 1] for c in range(PER_PART - 1)]]
+        att += [[att_rest[:, d, c : c + 1] for c in range(PER_PART)] for d in range(D - 1)]
+        spread(0, False, "bank_a")
+        quantize_w(0, [0], staged[0][:])
+        quantize_w(0, [1], staged[1][:])
         staged_1 = keep.tile([P, PASSES * K_PASS], BF16, name="w_bf_1", tag="w_bf_0_1", align_bytes=64)
         for g in range(PASSES):
             cast_w(1, g, staged_1[:, g * K_PASS : (g + 1) * K_PASS])
-        quantize_w(1, [0, 1], staged_1)
-        spread(0, False, "bank_a")
+            quantize_w(1, [g], staged_1[:, g * K_PASS : (g + 1) * K_PASS])
         project(0, [(0, "bank_b"), (1, "bank_c")])
         spread(1, False, "bank_b")
         spread(2, False, "bank_c")
-        project(1, [(0, "bank_a")])
-        project(1, [(1, "bank_b")])
 
         sum0 = psum.tile([P, T], F32, name="sum0", tag="sum0")
         term = gather(0, 0, 0, T)
+        project(1, [(0, "bank_a"), (1, "bank_e")])
         add_turned(sum0, term, True, False)
         term = gather(0, 1, 0, T)
         add_turned(sum0, term, False, False)

@@ -4,8 +4,9 @@ import concourse.mybir as mybir
 from concourse.masks import make_identity
 
 K, T, D, N = 1024, 512, 3, 256
+P = 128
 FLOPS = 2 * K * N * T
-BYTES = K * T + K * T // 32 + 4 * K * N + 4 * D * T + 2 * D * 128 * T // 16 + 4 * N * T
+BYTES = K * T + K * T // 32 + 4 * K * N + 4 * D * T + 2 * D * P * T // 16 + 4 * N * T
 
 F32 = mybir.dt.float32
 BF16 = mybir.dt.bfloat16
@@ -18,13 +19,17 @@ ALU = mybir.AluOpType
 ACT = mybir.ActivationFunctionType
 AXIS_X = mybir.AxisListType.X
 
-P = 128
 PACK = 4
 K_PASS = P * PACK
 PASSES = K // K_PASS
+BLOCKS = N // P
 HALF = T // 2
 SPARE = 16
 PER_PART = T // P
+QUADRANT = 32
+SCALE_ROWS = 4
+LIST_ROWS = 16
+RUN = 4
 
 
 def tile_picked_wgatv_none_l_kernel(
@@ -35,15 +40,15 @@ def tile_picked_wgatv_none_l_kernel(
         keep = ctx.enter_context(tc.tile_pool(name="keep", bufs=1))
         psum = ctx.enter_context(tc.psum_pool(name="psum", bufs=1))
 
-        sc = keep.tile([P, D, PER_PART], F32, name="sc")
-        nc.sync.dma_start(out=sc[:], in_=score[:, 0, :].rearrange("d (p c) -> p d c", c=PER_PART))
+        scores = keep.tile([P, D, PER_PART], F32, name="scores")
+        nc.sync.dma_start(out=scores[:], in_=score[:, 0, :].rearrange("d (p c) -> p d c", c=PER_PART))
 
-        x_plane = keep.tile([P, PASSES, T], U8, name="x_plane", align_bytes=64)
-        nc.gpsimd.memset(x_plane[:].bitcast(I32), 0)
-        plane_rows = x_scales.rearrange("g (q r) c -> r q g c", r=4)
+        x_scale_tile = keep.tile([P, PASSES, T], U8, name="x_scale_tile", align_bytes=64)
+        nc.gpsimd.memset(x_scale_tile[:].bitcast(I32), 0)
+        scale_rows = x_scales.rearrange("g (q r) c -> r q g c", r=SCALE_ROWS)
 
         w_raw = {}
-        lists = [keep.tile([P, T // 16], U16, name="list_%d" % d) for d in range(D)]
+        lists = [keep.tile([P, T // LIST_ROWS], U16, name="list_%d" % d) for d in range(D)]
 
         def load_w(m, g):
             w_raw[m, g] = keep.tile([P, PACK, P], F32, name="w_raw_%d_%d" % (m, g))
@@ -51,13 +56,11 @@ def tile_picked_wgatv_none_l_kernel(
             nc.sync.dma_start(out=w_raw[m, g][:], in_=rows.rearrange("(p j) n -> p j n", j=PACK))
 
         load_w(0, 0)
-        for r in range(4):
-            nc.sync.dma_start(out=x_plane[r:P:32, :, :].bitcast(I32), in_=plane_rows[r].bitcast(I32))
+        for r in range(SCALE_ROWS):
+            nc.sync.dma_start(out=x_scale_tile[r:P:QUADRANT, :, :].bitcast(I32), in_=scale_rows[r].bitcast(I32))
         load_w(0, 1)
         x_codes = keep.tile([P, PASSES, T], U32, name="x_codes", align_bytes=64)
-        nc.sync.dma_start(
-            out=x_codes[:].bitcast(I32), in_=x_words.rearrange("g p n t -> p g (n t)").bitcast(I32)
-        )
+        nc.sync.dma_start(out=x_codes[:].bitcast(I32), in_=x_words.rearrange("g p n t -> p g (n t)").bitcast(I32))
         load_w(1, 0)
         load_w(1, 1)
         for d, pos in enumerate((pos1, pos2, pos3)):
@@ -66,158 +69,142 @@ def tile_picked_wgatv_none_l_kernel(
         ident = keep.tile([P, P], F32, name="ident")
         nc.vector.memset(ident[:], 0.0)
         make_identity(nc, ident[:], nomemset=True)
-        y = [keep.tile([P, T + SPARE], F32, name="y_%d" % m) for m in range(2)]
-        for m in range(2):
-            nc.vector.memset(y[m][:, T:], 0.0)
 
-        warm = keep.tile([P, 2], F32, name="warm")
-        nc.vector.memset(warm[:, 0:1], 0.0)
-        nc.scalar.activation(out=warm[:, 1:2], in_=warm[:, 0:1], func=ACT.Exp)
+        y = [keep.tile([P, T + SPARE], F32, name="y_%d" % m) for m in range(BLOCKS)]
+        nc.vector.memset(y[1][:, T:], 0.0)
+        nc.scalar.activation(out=y[0][:, T:], in_=y[1][:, T:], func=ACT.Exp)
 
-        mx = keep.tile([P, PER_PART], F32, name="mx")
-        nc.vector.tensor_reduce(out=mx[:], in_=sc[:].rearrange("p d c -> p c d"), axis=AXIS_X, op=ALU.max)
-        sh = keep.tile([P, D, PER_PART], F32, name="sh", tag="w_bf_0_0", align_bytes=64)
+        largest = keep.tile([P, PER_PART], F32, name="largest")
+        nc.vector.tensor_reduce(out=largest[:], in_=scores[:].rearrange("p d c -> p c d"), axis=AXIS_X, op=ALU.max)
+        shifted = keep.tile([P, D, PER_PART], F32, name="shifted", tag="stage_first", align_bytes=64)
         nc.vector.tensor_tensor(
-            out=sh[:], in0=sc[:], in1=mx[:].unsqueeze(1).to_broadcast([P, D, PER_PART]), op=ALU.subtract
+            out=shifted[:], in0=scores[:], in1=largest[:].unsqueeze(1).to_broadcast([P, D, PER_PART]), op=ALU.subtract
         )
-        ex = keep.tile([P, D, PER_PART], F32, name="ex")
-        nc.scalar.activation(out=ex[:], in_=sh[:], func=ACT.Exp)
-        den = keep.tile([P, PER_PART], F32, name="den")
-        nc.vector.tensor_reduce(out=den[:], in_=ex[:].rearrange("p d c -> p c d"), axis=AXIS_X, op=ALU.add)
-        rec = keep.tile([P, PER_PART], F32, name="rec", tag="w_codes_0_1", align_bytes=64)
-        nc.vector.reciprocal(out=rec[:], in_=den[:])
+        exps = keep.tile([P, D, PER_PART], F32, name="exps")
+        nc.scalar.activation(out=exps[:], in_=shifted[:], func=ACT.Exp)
+        total = keep.tile([P, PER_PART], F32, name="total")
+        nc.vector.tensor_reduce(out=total[:], in_=exps[:].rearrange("p d c -> p c d"), axis=AXIS_X, op=ALU.add)
+        inverse = keep.tile([P, PER_PART], F32, name="inverse", tag="w_codes_0_1", align_bytes=64)
+        nc.vector.reciprocal(out=inverse[:], in_=total[:])
 
         a_rows = [keep.tile([P, T], F32, name="a_rows_%d" % d) for d in range(D)]
 
-        def spread(d, on_vector, tag):
-            bank = psum.tile([P, PER_PART, P], F32, name="a_bank_%d" % d, tag=tag)
+        def spread(d, bank_tag):
+            bank = psum.tile([P, PER_PART, P], F32, name="a_bank_%d" % d, tag=bank_tag)
             for c in range(PER_PART):
-                nc.tensor.transpose(bank[:, c, :], att[d][c].to_broadcast([P, P]), ident[:])
-            dst = a_rows[d][:].rearrange("i (p c) -> i p c", c=PER_PART)
-            src = bank[:].rearrange("i c p -> i p c")
-            if on_vector:
-                nc.vector.tensor_copy(out=dst, in_=src)
-            else:
-                nc.scalar.copy(out=dst, in_=src)
+                nc.tensor.transpose(bank[:, c, :], a_cols[d][c].to_broadcast([P, P]), ident[:])
+            nc.scalar.copy(
+                out=a_rows[d][:].rearrange("i (p c) -> i p c", c=PER_PART), in_=bank[:].rearrange("i c p -> i p c")
+            )
 
         w_codes = {}
-        w_plane = {}
+        w_scale_tile = {}
 
-        def cast_w(m, g, dst):
-            dst = dst.rearrange("p (c i t) -> p c t i", i=4, t=PACK)
-            src = w_raw[m, g][:].rearrange("p t (c i) -> p c t i", i=4)
-            if m == 1:
-                nc.vector.tensor_copy(out=dst, in_=src)
-            else:
-                nc.scalar.copy(out=dst, in_=src)
+        def cast_w(m, g, staged, copy):
+            copy(
+                out=staged.rearrange("p (c i t) -> p c t i", i=RUN, t=PACK),
+                in_=w_raw[m, g][:].rearrange("p t (c i) -> p c t i", i=RUN),
+            )
 
-        def quantize_w(m, passes, staged):
-            name = "%d_%d" % (m, passes[0])
-            codes = keep.tile([P, len(passes) * P], U32, name="w_codes_" + name, tag="w_codes_" + name, align_bytes=64)
-            plane = keep.tile([P, len(passes) * P], U8, name="w_plane_" + name, align_bytes=64)
-            nc.vector.quantize_mx(out=codes[:].bitcast(FP8X4), scales=plane[:], in_=staged)
-            for j, g in enumerate(passes):
-                w_codes[m, g] = codes[:, j * P : (j + 1) * P]
-                w_plane[m, g] = plane[:, j * P : (j + 1) * P]
+        def quantize_w(m, g, staged):
+            name = "w_codes_%d_%d" % (m, g)
+            w_codes[m, g] = keep.tile([P, P], U32, name=name, tag=name, align_bytes=64)
+            w_scale_tile[m, g] = keep.tile([P, P], U8, name="w_scale_tile_%d_%d" % (m, g), align_bytes=64)
+            nc.vector.quantize_mx(out=w_codes[m, g][:].bitcast(FP8X4), scales=w_scale_tile[m, g][:], in_=staged)
 
-        def project(m, halves):
-            banks = {h: psum.tile([P, HALF], F32, name="y_bank_%d_%d" % (m, h), tag=tag) for h, tag in halves}
+        def project(m, bank_tags):
+            banks = {h: psum.tile([P, HALF], F32, name="y_bank_%d_%d" % (m, h), tag=tag) for h, tag in bank_tags}
             for g in range(PASSES):
                 for h in banks:
                     cols = slice(h * HALF, (h + 1) * HALF)
                     nc.tensor.matmul_mx(
                         out=banks[h][:],
-                        lhsT=w_codes[m, g].bitcast(FP8X4),
-                        lhsT_scale=w_plane[m, g],
+                        lhsT=w_codes[m, g][:].bitcast(FP8X4),
+                        lhsT_scale=w_scale_tile[m, g][:],
                         rhs=x_codes[:, g, cols].bitcast(FP8X4),
-                        rhs_scale=x_plane[:, g, cols],
+                        rhs_scale=x_scale_tile[:, g, cols],
                         start=(g == 0),
                         stop=(g == PASSES - 1),
                     )
             for h in banks:
-                cols = slice(h * HALF, (h + 1) * HALF)
-                if (m, h) == (0, 1):
-                    nc.vector.tensor_copy(out=y[m][:, cols], in_=banks[h][:])
-                else:
-                    nc.scalar.copy(out=y[m][:, cols], in_=banks[h][:])
+                nc.scalar.copy(out=y[m][:, h * HALF : (h + 1) * HALF], in_=banks[h][:])
 
         def gather(m, d, lo, hi):
             term = keep.tile([P, hi - lo], F32, name="term_%d_%d_%d" % (m, d, lo))
             nc.vector.tensor_tensor(
                 out=term[:],
-                in0=y[m][:].indirect(lists[d][:, lo // 16 : hi // 16]),
+                in0=y[m][:].indirect(lists[d][:, lo // LIST_ROWS : hi // LIST_ROWS]),
                 in1=a_rows[d][:, lo:hi],
                 op=ALU.mult,
             )
             return term
 
         def add_turned(bank, term, first, last):
-            chunks = term.shape[1] // P
-            for c in range(chunks):
+            for c in range(PER_PART):
                 nc.tensor.matmul(
                     out=bank[:, c * P : (c + 1) * P],
                     lhsT=term[:, c * P : (c + 1) * P],
                     rhs=ident[:],
                     is_transpose=True,
                     start=(first and c == 0),
-                    stop=(last and c == chunks - 1),
+                    stop=(last and c == PER_PART - 1),
                 )
 
-        def turn_back(bank, width, name, tag):
-            turned = keep.tile([P, width], F32, name="turned_" + name)
-            nc.scalar.copy(out=turned[:], in_=bank[:])
-            back = psum.tile([P, width], F32, name="back_" + name, tag=tag)
-            for c in range(width // P):
-                nc.tensor.transpose(back[:, c * P : (c + 1) * P], turned[:, c * P : (c + 1) * P], ident[:])
-            return back
-
-        staged = [
-            keep.tile([P, K_PASS], BF16, name="w_bf_0_%d" % g, tag="w_bf_0_%d" % g, align_bytes=64)
-            for g in range(PASSES)
+        staged_0 = [
+            keep.tile([P, K_PASS], BF16, name="staged_0_%d" % g, tag=tag, align_bytes=64)
+            for g, tag in enumerate(("stage_first", "stage_second"))
         ]
         for g in range(PASSES):
-            cast_w(0, g, staged[g][:])
-        att_lead = keep.tile([P, 1], F32, name="att_lead", tag="w_codes_0_0", align_bytes=64)
-        nc.vector.tensor_tensor(out=att_lead[:], in0=ex[:, 0, 0:1], in1=rec[:, 0:1], op=ALU.mult)
-        att_first = keep.tile([P, PER_PART - 1], F32, name="att_first")
-        nc.vector.tensor_tensor(out=att_first[:], in0=ex[:, 0, 1:], in1=rec[:, 1:], op=ALU.mult)
-        att_rest = keep.tile([P, D - 1, PER_PART], F32, name="att_rest")
+            cast_w(0, g, staged_0[g][:], nc.scalar.copy)
+        a_lead = keep.tile([P, 1], F32, name="a_lead", tag="w_codes_0_0", align_bytes=64)
+        nc.vector.tensor_tensor(out=a_lead[:], in0=exps[:, 0, 0:1], in1=inverse[:, 0:1], op=ALU.mult)
+        a_first = keep.tile([P, PER_PART - 1], F32, name="a_first")
+        nc.vector.tensor_tensor(out=a_first[:], in0=exps[:, 0, 1:], in1=inverse[:, 1:], op=ALU.mult)
+        a_rest = keep.tile([P, D - 1, PER_PART], F32, name="a_rest")
         nc.vector.tensor_tensor(
-            out=att_rest[:], in0=ex[:, 1:, :], in1=rec[:].unsqueeze(1).to_broadcast([P, D - 1, PER_PART]), op=ALU.mult
+            out=a_rest[:],
+            in0=exps[:, 1:, :],
+            in1=inverse[:].unsqueeze(1).to_broadcast([P, D - 1, PER_PART]),
+            op=ALU.mult,
         )
-        att = [[att_lead[:]] + [att_first[:, c : c + 1] for c in range(PER_PART - 1)]]
-        att += [[att_rest[:, d, c : c + 1] for c in range(PER_PART)] for d in range(D - 1)]
-        spread(0, False, "bank_a")
-        quantize_w(0, [0], staged[0][:])
-        quantize_w(0, [1], staged[1][:])
-        staged_1 = keep.tile([P, PASSES * K_PASS], BF16, name="w_bf_1", tag="w_bf_0_1", align_bytes=64)
+        a_cols = [[a_lead[:]] + [a_first[:, c : c + 1] for c in range(PER_PART - 1)]]
+        a_cols.extend([a_rest[:, d, c : c + 1] for c in range(PER_PART)] for d in range(D - 1))
+        spread(0, "bank_chain")
         for g in range(PASSES):
-            cast_w(1, g, staged_1[:, g * K_PASS : (g + 1) * K_PASS])
-            quantize_w(1, [g], staged_1[:, g * K_PASS : (g + 1) * K_PASS])
-        project(0, [(0, "bank_b"), (1, "bank_c")])
-        spread(1, False, "bank_b")
-        spread(2, False, "bank_c")
+            quantize_w(0, g, staged_0[g][:])
 
-        sum0 = psum.tile([P, T], F32, name="sum0", tag="sum0")
+        staged_1 = keep.tile([P, PASSES * K_PASS], BF16, name="staged_1", tag="stage_first", align_bytes=64)
+        for g in range(PASSES):
+            cast_w(1, g, staged_1[:, g * K_PASS : (g + 1) * K_PASS], nc.vector.tensor_copy)
+            quantize_w(1, g, staged_1[:, g * K_PASS : (g + 1) * K_PASS])
+
+        project(0, [(0, "bank_left"), (1, "bank_right")])
+        spread(1, "bank_chain")
+        spread(2, "bank_right")
+
         term = gather(0, 0, 0, T)
-        project(1, [(0, "bank_a"), (1, "bank_e")])
-        add_turned(sum0, term, True, False)
-        term = gather(0, 1, 0, T)
-        add_turned(sum0, term, False, False)
-        term = gather(0, 2, 0, T)
-        add_turned(sum0, term, False, True)
-        back0 = turn_back(sum0, T, "0", "bank_d")
-        res0 = keep.tile([P, T], F32, name="res0")
-        nc.scalar.copy(out=res0[:], in_=back0[:])
-        nc.scalar.dma_start(out=out[0:P, :], in_=res0[:])
+        project(1, [(0, "bank_chain")])
+        project(1, [(1, "bank_right")])
+        turned_sum = psum.tile([P, T], F32, name="turned_sum", tag="bank_chain")
+        add_turned(turned_sum, term, True, False)
+        for d in range(1, D):
+            add_turned(turned_sum, gather(0, d, 0, T), False, d == D - 1)
+        turned = keep.tile([P, T], F32, name="turned")
+        nc.scalar.copy(out=turned[:], in_=turned_sum[:])
+        upright = psum.tile([P, T], F32, name="upright", tag="bank_upright")
+        for c in range(PER_PART):
+            nc.tensor.transpose(upright[:, c * P : (c + 1) * P], turned[:, c * P : (c + 1) * P], ident[:])
+        result_0 = keep.tile([P, T], F32, name="result_0")
+        nc.scalar.copy(out=result_0[:], in_=upright[:])
+        nc.scalar.dma_start(out=out[0:P, :], in_=result_0[:])
 
-        terms = [gather(1, d, 0, T) for d in range(2)]
-        last = [gather(1, 2, 0, HALF)]
+        terms = [gather(1, d, 0, T) for d in range(D - 1)]
+        thirds = [gather(1, D - 1, 0, HALF)]
         pair = keep.tile([P, T], F32, name="pair")
         nc.vector.tensor_tensor(out=pair[:], in0=terms[0][:], in1=terms[1][:], op=ALU.add)
-        last.append(gather(1, 2, HALF, T))
+        thirds.append(gather(1, D - 1, HALF, T))
         for h in range(2):
             cols = slice(h * HALF, (h + 1) * HALF)
-            res1 = keep.tile([P, HALF], F32, name="res1_%d" % h)
-            nc.vector.tensor_tensor(out=res1[:], in0=pair[:, cols], in1=last[h][:], op=ALU.add)
-            nc.sync.dma_start(out=out[P : 2 * P, cols], in_=res1[:])
+            result_1 = keep.tile([P, HALF], F32, name="result_1_%d" % h)
+            nc.vector.tensor_tensor(out=result_1[:], in0=pair[:, cols], in1=thirds[h][:], op=ALU.add)
+            nc.sync.dma_start(out=out[P : 2 * P, cols], in_=result_1[:])

from contextlib import ExitStack

import concourse.mybir as mybir
from concourse.masks import make_identity

K, T, D, N = 1024, 512, 3, 256
P = 128
FLOPS = 2 * K * N * T
BYTES = K * T + K * T // 32 + 4 * K * N + 4 * D * T + 2 * D * P * T // 16 + 4 * N * T

F32 = mybir.dt.float32
BF16 = mybir.dt.bfloat16
I32 = mybir.dt.int32
U32 = mybir.dt.uint32
U16 = mybir.dt.uint16
U8 = mybir.dt.uint8
FP8X4 = mybir.dt.float8_e4m3fn_x4
ALU = mybir.AluOpType
ACT = mybir.ActivationFunctionType
AXIS_X = mybir.AxisListType.X

PACK = 4
K_PASS = P * PACK
PASSES = K // K_PASS
BLOCKS = N // P
HALF = T // 2
SPARE = 16
PER_PART = T // P
QUADRANT = 32
SCALE_ROWS = 4
LIST_ROWS = 16
RUN = 4


def tile_picked_wgatv_none_l_kernel(
    tc, x_words, x_scales, w1, score, pos1, pos2, pos3, out
):
    nc = tc.nc
    with ExitStack() as ctx:
        keep = ctx.enter_context(tc.tile_pool(name="keep", bufs=1))
        psum = ctx.enter_context(tc.psum_pool(name="psum", bufs=1))

        scores = keep.tile([P, D, PER_PART], F32, name="scores")
        nc.sync.dma_start(out=scores[:], in_=score[:, 0, :].rearrange("d (p c) -> p d c", c=PER_PART))

        x_scale_tile = keep.tile([P, PASSES, T], U8, name="x_scale_tile", align_bytes=64)
        nc.gpsimd.memset(x_scale_tile[:].bitcast(I32), 0)
        scale_rows = x_scales.rearrange("g (q r) c -> r q g c", r=SCALE_ROWS)

        w_raw = {}
        lists = [keep.tile([P, T // LIST_ROWS], U16, name="list_%d" % d) for d in range(D)]

        def load_w(m, g):
            w_raw[m, g] = keep.tile([P, PACK, P], F32, name="w_raw_%d_%d" % (m, g))
            rows = w1[g * K_PASS : (g + 1) * K_PASS, m * P : (m + 1) * P]
            nc.sync.dma_start(out=w_raw[m, g][:], in_=rows.rearrange("(p j) n -> p j n", j=PACK))

        load_w(0, 0)
        for r in range(SCALE_ROWS):
            nc.sync.dma_start(out=x_scale_tile[r:P:QUADRANT, :, :].bitcast(I32), in_=scale_rows[r].bitcast(I32))
        load_w(0, 1)
        x_codes = keep.tile([P, PASSES, T], U32, name="x_codes", align_bytes=64)
        nc.sync.dma_start(out=x_codes[:].bitcast(I32), in_=x_words.rearrange("g p n t -> p g (n t)").bitcast(I32))
        load_w(1, 0)
        load_w(1, 1)
        for d, pos in enumerate((pos1, pos2, pos3)):
            nc.sync.dma_start(lists[d][:], pos)

        ident = keep.tile([P, P], F32, name="ident")
        nc.vector.memset(ident[:], 0.0)
        make_identity(nc, ident[:], nomemset=True)

        y = [keep.tile([P, T + SPARE], F32, name="y_%d" % m) for m in range(BLOCKS)]
        nc.vector.memset(y[1][:, T:], 0.0)
        nc.scalar.activation(out=y[0][:, T:], in_=y[1][:, T:], func=ACT.Exp)

        largest = keep.tile([P, PER_PART], F32, name="largest")
        nc.vector.tensor_reduce(out=largest[:], in_=scores[:].rearrange("p d c -> p c d"), axis=AXIS_X, op=ALU.max)
        shifted = keep.tile([P, D, PER_PART], F32, name="shifted", tag="stage_first", align_bytes=64)
        nc.vector.tensor_tensor(
            out=shifted[:], in0=scores[:], in1=largest[:].unsqueeze(1).to_broadcast([P, D, PER_PART]), op=ALU.subtract
        )
        exps = keep.tile([P, D, PER_PART], F32, name="exps")
        nc.scalar.activation(out=exps[:], in_=shifted[:], func=ACT.Exp)
        total = keep.tile([P, PER_PART], F32, name="total")
        nc.vector.tensor_reduce(out=total[:], in_=exps[:].rearrange("p d c -> p c d"), axis=AXIS_X, op=ALU.add)
        inverse = keep.tile([P, PER_PART], F32, name="inverse", tag="w_codes_0_1", align_bytes=64)
        nc.vector.reciprocal(out=inverse[:], in_=total[:])

        a_rows = [keep.tile([P, T], F32, name="a_rows_%d" % d) for d in range(D)]

        def spread(d, bank_tag):
            bank = psum.tile([P, PER_PART, P], F32, name="a_bank_%d" % d, tag=bank_tag)
            for c in range(PER_PART):
                nc.tensor.transpose(bank[:, c, :], a_cols[d][c].to_broadcast([P, P]), ident[:])
            nc.scalar.copy(
                out=a_rows[d][:].rearrange("i (p c) -> i p c", c=PER_PART), in_=bank[:].rearrange("i c p -> i p c")
            )

        w_codes = {}
        w_scale_tile = {}

        def cast_w(m, g, staged, copy):
            copy(
                out=staged.rearrange("p (c i t) -> p c t i", i=RUN, t=PACK),
                in_=w_raw[m, g][:].rearrange("p t (c i) -> p c t i", i=RUN),
            )

        def quantize_w(m, g, staged):
            name = "w_codes_%d_%d" % (m, g)
            w_codes[m, g] = keep.tile([P, P], U32, name=name, tag=name, align_bytes=64)
            w_scale_tile[m, g] = keep.tile([P, P], U8, name="w_scale_tile_%d_%d" % (m, g), align_bytes=64)
            nc.vector.quantize_mx(out=w_codes[m, g][:].bitcast(FP8X4), scales=w_scale_tile[m, g][:], in_=staged)

        def project(m, bank_tags):
            banks = {h: psum.tile([P, HALF], F32, name="y_bank_%d_%d" % (m, h), tag=tag) for h, tag in bank_tags}
            for g in range(PASSES):
                for h in banks:
                    cols = slice(h * HALF, (h + 1) * HALF)
                    nc.tensor.matmul_mx(
                        out=banks[h][:],
                        lhsT=w_codes[m, g][:].bitcast(FP8X4),
                        lhsT_scale=w_scale_tile[m, g][:],
                        rhs=x_codes[:, g, cols].bitcast(FP8X4),
                        rhs_scale=x_scale_tile[:, g, cols],
                        start=(g == 0),
                        stop=(g == PASSES - 1),
                    )
            for h in banks:
                nc.scalar.copy(out=y[m][:, h * HALF : (h + 1) * HALF], in_=banks[h][:])

        def gather(m, d, lo, hi):
            term = keep.tile([P, hi - lo], F32, name="term_%d_%d_%d" % (m, d, lo))
            nc.vector.tensor_tensor(
                out=term[:],
                in0=y[m][:].indirect(lists[d][:, lo // LIST_ROWS : hi // LIST_ROWS]),
                in1=a_rows[d][:, lo:hi],
                op=ALU.mult,
            )
            return term

        def add_turned(bank, term, first, last):
            for c in range(PER_PART):
                nc.tensor.matmul(
                    out=bank[:, c * P : (c + 1) * P],
                    lhsT=term[:, c * P : (c + 1) * P],
                    rhs=ident[:],
                    is_transpose=True,
                    start=(first and c == 0),
                    stop=(last and c == PER_PART - 1),
                )

        staged_0 = [
            keep.tile([P, K_PASS], BF16, name="staged_0_%d" % g, tag=tag, align_bytes=64)
            for g, tag in enumerate(("stage_first", "stage_second"))
        ]
        for g in range(PASSES):
            cast_w(0, g, staged_0[g][:], nc.scalar.copy)
        a_lead = keep.tile([P, 1], F32, name="a_lead", tag="w_codes_0_0", align_bytes=64)
        nc.vector.tensor_tensor(out=a_lead[:], in0=exps[:, 0, 0:1], in1=inverse[:, 0:1], op=ALU.mult)
        a_first = keep.tile([P, PER_PART - 1], F32, name="a_first")
        nc.vector.tensor_tensor(out=a_first[:], in0=exps[:, 0, 1:], in1=inverse[:, 1:], op=ALU.mult)
        a_rest = keep.tile([P, D - 1, PER_PART], F32, name="a_rest")
        nc.vector.tensor_tensor(
            out=a_rest[:],
            in0=exps[:, 1:, :],
            in1=inverse[:].unsqueeze(1).to_broadcast([P, D - 1, PER_PART]),
            op=ALU.mult,
        )
        a_cols = [[a_lead[:]] + [a_first[:, c : c + 1] for c in range(PER_PART - 1)]]
        a_cols.extend([a_rest[:, d, c : c + 1] for c in range(PER_PART)] for d in range(D - 1))
        spread(0, "bank_chain")
        for g in range(PASSES):
            quantize_w(0, g, staged_0[g][:])

        staged_1 = keep.tile([P, PASSES * K_PASS], BF16, name="staged_1", tag="stage_first", align_bytes=64)
        for g in range(PASSES):
            cast_w(1, g, staged_1[:, g * K_PASS : (g + 1) * K_PASS], nc.vector.tensor_copy)
            quantize_w(1, g, staged_1[:, g * K_PASS : (g + 1) * K_PASS])

        project(0, [(0, "bank_left"), (1, "bank_right")])
        spread(1, "bank_chain")
        spread(2, "bank_right")

        term = gather(0, 0, 0, T)
        project(1, [(0, "bank_chain")])
        project(1, [(1, "bank_right")])
        turned_sum = psum.tile([P, T], F32, name="turned_sum", tag="bank_chain")
        add_turned(turned_sum, term, True, False)
        for d in range(1, D):
            add_turned(turned_sum, gather(0, d, 0, T), False, d == D - 1)
        turned = keep.tile([P, T], F32, name="turned")
        nc.scalar.copy(out=turned[:], in_=turned_sum[:])
        upright = psum.tile([P, T], F32, name="upright", tag="bank_upright")
        for c in range(PER_PART):
            nc.tensor.transpose(upright[:, c * P : (c + 1) * P], turned[:, c * P : (c + 1) * P], ident[:])
        result_0 = keep.tile([P, T], F32, name="result_0")
        nc.scalar.copy(out=result_0[:], in_=upright[:])
        nc.scalar.dma_start(out=out[0:P, :], in_=result_0[:])

        terms = [gather(1, d, 0, T) for d in range(D - 1)]
        thirds = [gather(1, D - 1, 0, HALF)]
        pair = keep.tile([P, T], F32, name="pair")
        nc.vector.tensor_tensor(out=pair[:], in0=terms[0][:], in1=terms[1][:], op=ALU.add)
        thirds.append(gather(1, D - 1, HALF, T))
        for h in range(2):
            cols = slice(h * HALF, (h + 1) * HALF)
            result_1 = keep.tile([P, HALF], F32, name="result_1_%d" % h)
            nc.vector.tensor_tensor(out=result_1[:], in0=pair[:, cols], in1=thirds[h][:], op=ALU.add)
            nc.sync.dma_start(out=out[P : 2 * P, cols], in_=result_1[:])
